import numpy as np
import ml_dtypes

BF16 = ml_dtypes.bfloat16


def bf(x):
    return np.asarray(x, np.float32).astype(BF16)


def f32(x):
    return np.asarray(x, np.float32)


def f64(x):
    return np.asarray(x).astype(np.float64)


def striped(idx):
    return np.concatenate([l.reshape(-1, 16).T for l in idx])


def rows(idx, k):
    return np.tile(np.repeat(idx, 16, axis=0), (k // (16 * 8), 1))


def look(tab, idx):
    return np.take_along_axis(f64(tab), rows(idx, len(tab)), axis=1)


K, S, V, N, M = 512, 2048, 2048, 2048, 128


def setup_inputs():
    return {"tab": f32(np.random.standard_normal((K, S))), "s": f32(np.random.uniform(0.5, 1.5, (K, 1))), "c": f32(0.3 * np.random.standard_normal((K, 1))), "w": bf(np.random.standard_normal((K, M)) / np.sqrt(K)), "b": f32(0.5 * np.random.standard_normal((M, 1))), "offs": striped(np.random.randint(0, S, (8, N)))}


def reference(tab, s, c, w, b, offs):
    idx = np.stack([g.T.reshape(-1) for g in np.split(offs, 8)])
    t = look(tab, idx)
    x = f64(s) * t + f64(c)
    y = f64(w).T @ x
    return np.maximum(y + f64(b), 0.0)

@@ -1,0 +1,69 @@
+import concourse.mybir as mybir
+
+F32, BF16, U16 = mybir.dt.float32, mybir.dt.bfloat16, mybir.dt.uint16
+MULT, ADD = mybir.AluOpType.mult, mybir.AluOpType.add
+RELU = mybir.ActivationFunctionType.Relu
+
+P = 128
+ROWS, COLUMNS, LIST = 512, 2048, 2048
+BLOCKS = ROWS // P
+PIECE = 512
+PIECES = LIST // PIECE
+PIECE_OFFS = PIECE // 16
+
+FLOPS = 2 * ROWS * P * LIST + 2 * ROWS * LIST
+
+
+def tile_lookup_deq_affp_relu_kernel(tc, tab, s, c, w, b, offs, out):
+    nc = tc.nc
+    with (
+        tc.tile_pool(name="held", bufs=1) as held,
+        tc.tile_pool(name="ring", bufs=4) as ring,
+        tc.psum_pool(name="psum", bufs=1) as psum,
+    ):
+        offsets = held.tile([P, LIST // 16], U16, name="offsets")
+        nc.sync.dma_start(offsets[:], offs)
+
+        scale = held.tile([P, BLOCKS], F32, name="scale")
+        shift = held.tile([P, BLOCKS], F32, name="shift")
+        bias = held.tile([P, 1], F32, name="bias")
+        with nc.allow_non_contiguous_dma(reason="one value for each partition"):
+            nc.scalar.dma_start(scale[:], s.rearrange("(r p) o -> p (r o)", p=P))
+            nc.scalar.dma_start(shift[:], c.rearrange("(r p) o -> p (r o)", p=P))
+        weights = held.tile([P, BLOCKS, P], BF16, name="weights")
+        nc.scalar.dma_start(weights[:], w.rearrange("(r p) m -> p r m", p=P))
+        nc.scalar.dma_start(bias[:], b)
+
+        windows = []
+        for r in range(BLOCKS):
+            window = held.tile([P, COLUMNS], F32, name=f"window{r}")
+            nc.sync.dma_start(window[:], tab[r * P : (r + 1) * P, :])
+            windows.append(window)
+
+        sums = [psum.tile([P, PIECE], F32, name=f"sum{j}") for j in range(PIECES)]
+
+        for r in range(BLOCKS):
+            for j in range(PIECES):
+                x = ring.tile([P, PIECE], F32, name="x")
+                nc.vector.tensor_scalar(
+                    x[:],
+                    windows[r][:].indirect(offsets[:, j * PIECE_OFFS : (j + 1) * PIECE_OFFS]),
+                    scale[:, r : r + 1],
+                    shift[:, r : r + 1],
+                    MULT,
+                    ADD,
+                )
+                x_rounded = ring.tile([P, PIECE], BF16, name="x_rounded")
+                nc.scalar.copy(x_rounded[:], x[:])
+                nc.tensor.matmul(
+                    sums[j][:],
+                    weights[:, r, :],
+                    x_rounded[:],
+                    start=(r == 0),
+                    stop=(r == BLOCKS - 1),
+                )
+
+        for j in range(PIECES):
+            result = ring.tile([P, PIECE], F32, name="result")
+            nc.scalar.activation(result[:], sums[j][:], RELU, bias=bias[:])
+            nc.sync.dma_start(out[:, j * PIECE : (j + 1) * PIECE], result[:])

@@ -1,7 +1,7 @@
 import concourse.mybir as mybir
 
 F32, BF16, U16 = mybir.dt.float32, mybir.dt.bfloat16, mybir.dt.uint16
-MULT, ADD = mybir.AluOpType.mult, mybir.AluOpType.add
+MULT, ADD, MAX = mybir.AluOpType.mult, mybir.AluOpType.add, mybir.AluOpType.max
 RELU = mybir.ActivationFunctionType.Relu
 
 P = 128
@@ -40,30 +40,48 @@ def tile_lookup_deq_affp_relu_kernel(tc, tab, s, c, w, b, offs, out):
             nc.sync.dma_start(window[:], tab[r * P : (r + 1) * P, :])
             windows.append(window)
 
-        sums = [psum.tile([P, PIECE], F32, name=f"sum{j}") for j in range(PIECES)]
+        sums = []
+        for j in range(PIECES):
+            parts = 2 if j == PIECES - 1 else 1
+            sums.append(
+                [psum.tile([P, PIECE // parts], F32, name=f"sum{j}_{h}") for h in range(parts)]
+            )
 
-        for r in range(BLOCKS):
-            for j in range(PIECES):
-                x = ring.tile([P, PIECE], F32, name="x")
-                nc.vector.tensor_scalar(
-                    x[:],
-                    windows[r][:].indirect(offsets[:, j * PIECE_OFFS : (j + 1) * PIECE_OFFS]),
-                    scale[:, r : r + 1],
-                    shift[:, r : r + 1],
-                    MULT,
-                    ADD,
-                )
-                x_rounded = ring.tile([P, PIECE], BF16, name="x_rounded")
+        early, late = range(BLOCKS // 2), range(BLOCKS // 2, BLOCKS)
+        order = [(r, j) for r in early for j in range(PIECES)]
+        order += [(r, j) for j in range(PIECES) for r in late]
+
+        for r, j in order:
+            x = ring.tile([P, PIECE], F32, name="x")
+            nc.vector.tensor_scalar(
+                x[:],
+                windows[r][:].indirect(offsets[:, j * PIECE_OFFS : (j + 1) * PIECE_OFFS]),
+                scale[:, r : r + 1],
+                shift[:, r : r + 1],
+                MULT,
+                ADD,
+            )
+            x_rounded = ring.tile([P, PIECE], BF16, name="x_rounded")
+            width = PIECE // len(sums[j])
+            if (r, j) == order[-1]:
+                nc.scalar.copy(x_rounded[:, :width], x[:, :width])
+                nc.vector.tensor_copy(x_rounded[:, width:], x[:, width:])
+            else:
                 nc.scalar.copy(x_rounded[:], x[:])
+            for h, total in enumerate(sums[j]):
                 nc.tensor.matmul(
-                    sums[j][:],
+                    total[:],
                     weights[:, r, :],
-                    x_rounded[:],
+                    x_rounded[:, h * width : (h + 1) * width],
                     start=(r == 0),
                     stop=(r == BLOCKS - 1),
                 )
-
-        for j in range(PIECES):
-            result = ring.tile([P, PIECE], F32, name="result")
-            nc.scalar.activation(result[:], sums[j][:], RELU, bias=bias[:])
-            nc.sync.dma_start(out[:, j * PIECE : (j + 1) * PIECE], result[:])
+            if r == BLOCKS - 1:
+                for h, total in enumerate(sums[j]):
+                    result = ring.tile([P, width], F32, name=f"result_{width}")
+                    if h == 0:
+                        nc.scalar.activation(result[:], total[:], RELU, bias=bias[:])
+                    else:
+                        nc.vector.tensor_scalar(result[:], total[:], bias[:], 0.0, ADD, MAX)
+                    first = j * PIECE + h * width
+                    nc.sync.dma_start(out[:, first : first + width], result[:])

@@ -24,21 +24,24 @@ def tile_lookup_deq_affp_relu_kernel(tc, tab, s, c, w, b, offs, out):
         offsets = held.tile([P, LIST // 16], U16, name="offsets")
         nc.sync.dma_start(offsets[:], offs)
 
-        scale = held.tile([P, BLOCKS], F32, name="scale")
-        shift = held.tile([P, BLOCKS], F32, name="shift")
-        bias = held.tile([P, 1], F32, name="bias")
-        with nc.allow_non_contiguous_dma(reason="one value for each partition"):
-            nc.scalar.dma_start(scale[:], s.rearrange("(r p) o -> p (r o)", p=P))
-            nc.scalar.dma_start(shift[:], c.rearrange("(r p) o -> p (r o)", p=P))
-        weights = held.tile([P, BLOCKS, P], BF16, name="weights")
-        nc.scalar.dma_start(weights[:], w.rearrange("(r p) m -> p r m", p=P))
-        nc.scalar.dma_start(bias[:], b)
-
-        windows = []
+        windows, scales, shifts = [], [], []
         for r in range(BLOCKS):
+            block = slice(r * P, (r + 1) * P)
+            queue = nc.scalar if r == 0 else nc.sync
+            scale = held.tile([P, 1], F32, name=f"scale{r}")
+            queue.dma_start(scale[:], s[block, :])
+            shift = held.tile([P, 1], F32, name=f"shift{r}")
+            queue.dma_start(shift[:], c[block, :])
             window = held.tile([P, COLUMNS], F32, name=f"window{r}")
-            nc.sync.dma_start(window[:], tab[r * P : (r + 1) * P, :])
+            nc.sync.dma_start(window[:], tab[block, :])
             windows.append(window)
+            scales.append(scale)
+            shifts.append(shift)
+            if r == 0:
+                weights = held.tile([P, BLOCKS, P], BF16, name="weights")
+                nc.sync.dma_start(weights[:], w.rearrange("(r p) m -> p r m", p=P))
+                bias = held.tile([P, 1], F32, name="bias")
+                nc.sync.dma_start(bias[:], b)
 
         sums = []
         for j in range(PIECES):
@@ -56,8 +59,8 @@ def tile_lookup_deq_affp_relu_kernel(tc, tab, s, c, w, b, offs, out):
             nc.vector.tensor_scalar(
                 x[:],
                 windows[r][:].indirect(offsets[:, j * PIECE_OFFS : (j + 1) * PIECE_OFFS]),
-                scale[:, r : r + 1],
-                shift[:, r : r + 1],
+                scales[r][:],
+                shifts[r][:],
                 MULT,
                 ADD,
             )

import concourse.mybir as mybir

F32, BF16, U16 = mybir.dt.float32, mybir.dt.bfloat16, mybir.dt.uint16
MULT, ADD, MAX = mybir.AluOpType.mult, mybir.AluOpType.add, mybir.AluOpType.max
RELU = mybir.ActivationFunctionType.Relu

P = 128
ROWS, COLUMNS, LIST = 512, 2048, 2048
BLOCKS = ROWS // P
PIECE = 512
PIECES = LIST // PIECE
PIECE_OFFS = PIECE // 16

FLOPS = 2 * ROWS * P * LIST + 2 * ROWS * LIST


def tile_lookup_deq_affp_relu_kernel(tc, tab, s, c, w, b, offs, out):
    nc = tc.nc
    with (
        tc.tile_pool(name="held", bufs=1) as held,
        tc.tile_pool(name="ring", bufs=4) as ring,
        tc.psum_pool(name="psum", bufs=1) as psum,
    ):
        offsets = held.tile([P, LIST // 16], U16, name="offsets")
        nc.sync.dma_start(offsets[:], offs)

        windows, scales, shifts = [], [], []
        for r in range(BLOCKS):
            block = slice(r * P, (r + 1) * P)
            queue = nc.scalar if r == 0 else nc.sync
            scale = held.tile([P, 1], F32, name=f"scale{r}")
            queue.dma_start(scale[:], s[block, :])
            shift = held.tile([P, 1], F32, name=f"shift{r}")
            queue.dma_start(shift[:], c[block, :])
            window = held.tile([P, COLUMNS], F32, name=f"window{r}")
            nc.sync.dma_start(window[:], tab[block, :])
            windows.append(window)
            scales.append(scale)
            shifts.append(shift)
            if r == 0:
                weights = held.tile([P, BLOCKS, P], BF16, name="weights")
                nc.sync.dma_start(weights[:], w.rearrange("(r p) m -> p r m", p=P))
                bias = held.tile([P, 1], F32, name="bias")
                nc.sync.dma_start(bias[:], b)

        sums = []
        for j in range(PIECES):
            parts = 2 if j == PIECES - 1 else 1
            sums.append(
                [psum.tile([P, PIECE // parts], F32, name=f"sum{j}_{h}") for h in range(parts)]
            )

        early, late = range(BLOCKS // 2), range(BLOCKS // 2, BLOCKS)
        order = [(r, j) for r in early for j in range(PIECES)]
        order += [(r, j) for j in range(PIECES) for r in late]

        for r, j in order:
            x = ring.tile([P, PIECE], F32, name="x")
            nc.vector.tensor_scalar(
                x[:],
                windows[r][:].indirect(offsets[:, j * PIECE_OFFS : (j + 1) * PIECE_OFFS]),
                scales[r][:],
                shifts[r][:],
                MULT,
                ADD,
            )
            x_rounded = ring.tile([P, PIECE], BF16, name="x_rounded")
            width = PIECE // len(sums[j])
            if (r, j) == order[-1]:
                nc.scalar.copy(x_rounded[:, :width], x[:, :width])
                nc.vector.tensor_copy(x_rounded[:, width:], x[:, width:])
            else:
                nc.scalar.copy(x_rounded[:], x[:])
            for h, total in enumerate(sums[j]):
                nc.tensor.matmul(
                    total[:],
                    weights[:, r, :],
                    x_rounded[:, h * width : (h + 1) * width],
                    start=(r == 0),
                    stop=(r == BLOCKS - 1),
                )
            if r == BLOCKS - 1:
                for h, total in enumerate(sums[j]):
                    result = ring.tile([P, width], F32, name=f"result_{width}")
                    if h == 0:
                        nc.scalar.activation(result[:], total[:], RELU, bias=bias[:])
                    else:
                        nc.vector.tensor_scalar(result[:], total[:], bias[:], 0.0, ADD, MAX)
                    first = j * PIECE + h * width
                    nc.sync.dma_start(out[:, first : first + width], result[:])
